import numpy as np
import ml_dtypes


def mxq(x, axis, fmt="e4m3"):
    dtype, down = {"e4m3": (ml_dtypes.float8_e4m3fn, 7), "e5m2": (ml_dtypes.float8_e5m2, 14)}[fmt]
    v = np.moveaxis(np.asarray(x, np.float32).astype(ml_dtypes.bfloat16).astype(np.float64), axis, -1)
    blocks = v.reshape(v.shape[:-1] + (-1, 32))
    amax = np.abs(blocks).max(-1, keepdims=True)
    byte = np.maximum(np.where(amax > 0, np.frexp(amax)[1] - 1 + 127, 0) - down, 1)
    scale = np.exp2(byte - 127.0)
    codes = (blocks / scale).astype(np.float32).astype(dtype).astype(np.float64)
    return np.moveaxis((codes * scale).reshape(v.shape), -1, axis)


WIDE = False


def mx_kscale(k):
    if not WIDE:
        return np.ones(k)
    levels = np.array([10, -10, 5, -5, 0])
    if k % 512:
        return np.exp2(np.random.permutation(np.resize(levels, k // 32))).repeat(32)
    a = np.empty((k // 512, 16))
    for p in range(k // 512):
        a[p, :8] = np.random.permutation(np.resize(levels, 8))
        for g in range(8):
            far = levels[np.abs(levels - a[p, g]) >= 10]
            a[p, g + 8] = far[np.random.randint(len(far))]
    return np.exp2(a.ravel()).repeat(32)


def f64(x):
    return np.asarray(x).astype(np.float64)


def striped8(idx):
    return np.concatenate([x.reshape(-1, 16).T for x in idx]).astype(np.uint16)


def runs(offs, k):
    lists = np.stack([offs[16 * r : 16 * r + 16].T.reshape(-1) for r in range(8)]).astype(np.int64)
    return lists[np.arange(k) % 512 // 64]


def pack_weight(w):
    k, n = w.shape
    w = f64(np.asarray(w, np.float32).astype(ml_dtypes.bfloat16)).reshape(k // 32, 32, n)
    amax = np.abs(w).max(1)
    byte = np.clip(np.where(amax > 0, np.frexp(amax)[1] - 1 + 127 - 7, 1), 1, 254)
    scaled = (w * np.exp2(127.0 - byte)[:, None, :]).reshape(k, n).astype(np.float32)
    words = np.ascontiguousarray(scaled.reshape(k // 512, 128, 4, n).transpose(0, 1, 3, 2)).astype(ml_dtypes.float8_e4m3fn).view(np.uint8)
    return words, np.ascontiguousarray(byte.astype(np.uint8).reshape(k // 512, 16, n))


def unpack_weight(words, scales):
    g, p, n, _ = words.shape
    vals = np.ascontiguousarray(words).view(ml_dtypes.float8_e4m3fn).astype(np.float64) * np.repeat(np.exp2(scales.astype(np.float64) - 127.0), 8, axis=1)[..., None]
    return vals.transpose(0, 1, 3, 2).reshape(g * 512, n)


K, T, S, N = 1024, 2048, 512, 128


def setup_inputs():
    n = np.random.standard_normal
    s = mx_kscale(K)[:, None]
    packed_xT = pack_weight(n((K, T)) * s)
    return {
        "x_words": packed_xT[0],
        "x_scales": packed_xT[1],
        "w1": (n((K, N)) / np.sqrt(K) / s).astype(np.float32),
        "res": n((N, S)).astype(np.float32),
        "gate": np.random.uniform(0.3, 1.2, (N, 1)).astype(np.float32),
        "offs": striped8(np.stack([np.random.permutation(T)[:S] for _ in range(8)])),
    }


def reference(x_words, x_scales, w1, res, gate, offs):
    xq = unpack_weight(x_words, x_scales)[np.arange(K)[:, None], runs(offs, K)]
    return f64(res) + f64(gate) * ((mxq(f64(w1), 0, "e4m3").T @ xq))

@@ -1,0 +1,103 @@
+from contextlib import ExitStack
+
+import concourse.mybir as mybir
+
+K, T, S, N = 1024, 2048, 512, 128
+FLOPS = 2 * K * S * N
+
+F32 = mybir.dt.float32
+BF16 = mybir.dt.bfloat16
+I32 = mybir.dt.int32
+U32 = mybir.dt.uint32
+U16 = mybir.dt.uint16
+U8 = mybir.dt.uint8
+FP8X4 = mybir.dt.float8_e4m3fn_x4
+MULT = mybir.AluOpType.mult
+ADD = mybir.AluOpType.add
+
+P = 128
+PACK = 4
+PASSES = K // (P * PACK)
+HALF = S // 2
+
+
+def tile_picked_phout_none_p_kernel(tc, x_words, x_scales, w1, res, gate, offs, out):
+    nc = tc.nc
+    with ExitStack() as ctx:
+        keep = ctx.enter_context(tc.tile_pool(name="keep", bufs=1))
+        psum = ctx.enter_context(tc.psum_pool(name="psum", bufs=1))
+
+        offsets = keep.tile([P, S // 16], U16, name="offsets")
+        w_raw = keep.tile([P, PASSES, PACK, N], F32, name="w_raw")
+        word_win = [keep.tile([P, T], I32, name="word_win%d" % z, align_bytes=64) for z in range(PASSES)]
+        res_sb = keep.tile([P, S], F32, name="res_sb")
+        gate_sb = keep.tile([P, 1], F32, name="gate_sb")
+        scale_win = keep.tile([P, T], U8, name="scale_win", align_bytes=64)
+        scale_got = keep.tile([P, S], U8, name="scale_got", align_bytes=64)
+        x_planes = keep.tile([P, PASSES * S], U8, name="x_planes", align_bytes=64)
+
+        nc.vector.memset(scale_win[:].bitcast(I32), 0)
+        nc.gpsimd.memset(x_planes[:].bitcast(I32), 0)
+
+        nc.sync.dma_start(w_raw[:], w1.rearrange("(z p j) m -> p z j m", z=PASSES, j=PACK))
+        nc.sync.dma_start(
+            scale_win[0:P:4, :].bitcast(I32),
+            x_scales.bitcast(I32).rearrange("z q c -> q z c"),
+        )
+        nc.sync.dma_start(offsets[:], offs)
+        for z in range(PASSES):
+            nc.sync.dma_start(word_win[z][:], x_words[z].rearrange("p c r -> p (c r)").bitcast(I32))
+        nc.sync.dma_start(gate_sb[:], gate)
+        nc.sync.dma_start(res_sb[:], res)
+
+        nc.vector.tensor_copy(scale_got[:], scale_win[:].indirect(offsets[:]))
+        for q in range(4):
+            nc.scalar.dma_start(
+                x_planes[32 * q : 32 * q + 4, :].bitcast(I32),
+                scale_got[32 * q : 32 * q + 32 : 4, :].bitcast(I32),
+            )
+
+        w_bf = keep.tile([P, PASSES, N, PACK], BF16, name="w_bf", align_bytes=64)
+        w_codes = keep.tile([P, PASSES * N], U32, name="w_codes", align_bytes=64)
+        w_planes = keep.tile([P, PASSES * N], U8, name="w_planes", align_bytes=64)
+        nc.vector.tensor_copy(w_bf[:], w_raw[:].rearrange("p z j m -> p z m j"))
+        nc.vector.quantize_mx(
+            out=w_codes[:].bitcast(FP8X4),
+            scales=w_planes[:],
+            in_=w_bf[:].rearrange("p z m j -> p (z m j)"),
+        )
+
+        got0 = keep.tile([P, S], U32, name="got0", align_bytes=64)
+        got1 = [keep.tile([P, HALF], U32, name="got1_%d" % h, align_bytes=64) for h in range(2)]
+        acc = [psum.tile([P, HALF], F32, name="acc%d" % h) for h in range(2)]
+        result = [keep.tile([P, HALF], F32, name="result%d" % h) for h in range(2)]
+
+        nc.vector.tensor_copy(got0[:], word_win[0][:].bitcast(U32).indirect(offsets[:]))
+        for h in range(2):
+            nc.tensor.matmul_mx(
+                out=acc[h][:],
+                lhsT=w_codes[:, 0:N].bitcast(FP8X4),
+                lhsT_scale=w_planes[:, 0:N],
+                rhs=got0[:, h * HALF : (h + 1) * HALF].bitcast(FP8X4),
+                rhs_scale=x_planes[:, h * HALF : (h + 1) * HALF],
+                start=True,
+                stop=False,
+            )
+        for h in range(2):
+            nc.vector.tensor_copy(
+                got1[h][:], word_win[1][:].bitcast(U32).indirect(offsets[:, h * 16 : (h + 1) * 16])
+            )
+            nc.tensor.matmul_mx(
+                out=acc[h][:],
+                lhsT=w_codes[:, N : 2 * N].bitcast(FP8X4),
+                lhsT_scale=w_planes[:, N : 2 * N],
+                rhs=got1[h][:].bitcast(FP8X4),
+                rhs_scale=x_planes[:, S + h * HALF : S + (h + 1) * HALF],
+                start=False,
+                stop=True,
+            )
+        for h in range(2):
+            cols = slice(h * HALF, (h + 1) * HALF)
+            nc.vector.scalar_tensor_tensor(result[h][:], acc[h][:], gate_sb[:], res_sb[:, cols], MULT, ADD)
+            queue = nc.sync if h == 0 else nc.scalar
+            queue.dma_start(out[:, cols], result[h][:])

@@ -28,27 +28,26 @@ def tile_picked_phout_none_p_kernel(tc, x_words, x_scales, w1, res, gate, offs, 
         psum = ctx.enter_context(tc.psum_pool(name="psum", bufs=1))
 
         offsets = keep.tile([P, S // 16], U16, name="offsets")
-        w_raw = keep.tile([P, PASSES, PACK, N], F32, name="w_raw")
+        w_raw = keep.tile([P, PASSES, PACK, N], F32, name="w_raw", tag="stage")
         word_win = [keep.tile([P, T], I32, name="word_win%d" % z, align_bytes=64) for z in range(PASSES)]
-        res_sb = keep.tile([P, S], F32, name="res_sb")
-        gate_sb = keep.tile([P, 1], F32, name="gate_sb")
         scale_win = keep.tile([P, T], U8, name="scale_win", align_bytes=64)
         scale_got = keep.tile([P, S], U8, name="scale_got", align_bytes=64)
         x_planes = keep.tile([P, PASSES * S], U8, name="x_planes", align_bytes=64)
 
-        nc.vector.memset(scale_win[:].bitcast(I32), 0)
-        nc.gpsimd.memset(x_planes[:].bitcast(I32), 0)
+        nc.vector.memset(scale_win[:, 0 : T // 2].bitcast(I32), 0)
+        nc.gpsimd.memset(scale_win[:, T // 2 : T].bitcast(I32), 0)
+        nc.vector.memset(x_planes[:].bitcast(I32), 0)
 
-        nc.sync.dma_start(w_raw[:], w1.rearrange("(z p j) m -> p z j m", z=PASSES, j=PACK))
+        w_rows = w1.rearrange("(z p j) m -> z p j m", z=PASSES, j=PACK)
+        nc.sync.dma_start(w_raw[:, 0], w_rows[0])
+        nc.sync.dma_start(offsets[:], offs)
         nc.sync.dma_start(
             scale_win[0:P:4, :].bitcast(I32),
             x_scales.bitcast(I32).rearrange("z q c -> q z c"),
         )
-        nc.sync.dma_start(offsets[:], offs)
+        nc.sync.dma_start(w_raw[:, 1], w_rows[1])
         for z in range(PASSES):
             nc.sync.dma_start(word_win[z][:], x_words[z].rearrange("p c r -> p (c r)").bitcast(I32))
-        nc.sync.dma_start(gate_sb[:], gate)
-        nc.sync.dma_start(res_sb[:], res)
 
         nc.vector.tensor_copy(scale_got[:], scale_win[:].indirect(offsets[:]))
         for q in range(4):
@@ -67,6 +66,10 @@ def tile_picked_phout_none_p_kernel(tc, x_words, x_scales, w1, res, gate, offs, 
             in_=w_bf[:].rearrange("p z m j -> p (z m j)"),
         )
 
+        res_gate = keep.tile([P, S + 8], F32, name="res_gate", tag="stage")
+        nc.sync.dma_start(res_gate[:, S : S + 1], gate)
+        nc.sync.dma_start(res_gate[:, 0:S], res)
+
         got0 = keep.tile([P, S], U32, name="got0", align_bytes=64)
         got1 = [keep.tile([P, HALF], U32, name="got1_%d" % h, align_bytes=64) for h in range(2)]
         acc = [psum.tile([P, HALF], F32, name="acc%d" % h) for h in range(2)]
@@ -74,30 +77,23 @@ def tile_picked_phout_none_p_kernel(tc, x_words, x_scales, w1, res, gate, offs, 
 
         nc.vector.tensor_copy(got0[:], word_win[0][:].bitcast(U32).indirect(offsets[:]))
         for h in range(2):
-            nc.tensor.matmul_mx(
-                out=acc[h][:],
-                lhsT=w_codes[:, 0:N].bitcast(FP8X4),
-                lhsT_scale=w_planes[:, 0:N],
-                rhs=got0[:, h * HALF : (h + 1) * HALF].bitcast(FP8X4),
-                rhs_scale=x_planes[:, h * HALF : (h + 1) * HALF],
-                start=True,
-                stop=False,
-            )
-        for h in range(2):
             nc.vector.tensor_copy(
                 got1[h][:], word_win[1][:].bitcast(U32).indirect(offsets[:, h * 16 : (h + 1) * 16])
             )
-            nc.tensor.matmul_mx(
-                out=acc[h][:],
-                lhsT=w_codes[:, N : 2 * N].bitcast(FP8X4),
-                lhsT_scale=w_planes[:, N : 2 * N],
-                rhs=got1[h][:].bitcast(FP8X4),
-                rhs_scale=x_planes[:, S + h * HALF : S + (h + 1) * HALF],
-                start=False,
-                stop=True,
-            )
+        for h in range(2):
+            for z in range(PASSES):
+                codes = got0[:, h * HALF : (h + 1) * HALF] if z == 0 else got1[h][:]
+                nc.tensor.matmul_mx(
+                    out=acc[h][:],
+                    lhsT=w_codes[:, z * N : (z + 1) * N].bitcast(FP8X4),
+                    lhsT_scale=w_planes[:, z * N : (z + 1) * N],
+                    rhs=codes.bitcast(FP8X4),
+                    rhs_scale=x_planes[:, z * S + h * HALF : z * S + (h + 1) * HALF],
+                    start=(z == 0),
+                    stop=(z == PASSES - 1),
+                )
         for h in range(2):
             cols = slice(h * HALF, (h + 1) * HALF)
-            nc.vector.scalar_tensor_tensor(result[h][:], acc[h][:], gate_sb[:], res_sb[:, cols], MULT, ADD)
+            nc.vector.scalar_tensor_tensor(result[h][:], acc[h][:], res_gate[:, S : S + 1], res_gate[:, cols], MULT, ADD)
             queue = nc.sync if h == 0 else nc.scalar
             queue.dma_start(out[:, cols], result[h][:])

@@ -80,8 +80,8 @@ def tile_picked_phout_none_p_kernel(tc, x_words, x_scales, w1, res, gate, offs, 
             nc.vector.tensor_copy(
                 got1[h][:], word_win[1][:].bitcast(U32).indirect(offsets[:, h * 16 : (h + 1) * 16])
             )
-        for h in range(2):
-            for z in range(PASSES):
+        for z in range(PASSES):
+            for h in range(2):
                 codes = got0[:, h * HALF : (h + 1) * HALF] if z == 0 else got1[h][:]
                 nc.tensor.matmul_mx(
                     out=acc[h][:],

@@ -19,6 +19,7 @@ P = 128
 PACK = 4
 PASSES = K // (P * PACK)
 HALF = S // 2
+EARLY = 3 * T // 4
 
 
 def tile_picked_phout_none_p_kernel(tc, x_words, x_scales, w1, res, gate, offs, out):
@@ -46,15 +47,17 @@ def tile_picked_phout_none_p_kernel(tc, x_words, x_scales, w1, res, gate, offs, 
             x_scales.bitcast(I32).rearrange("z q c -> q z c"),
         )
         nc.sync.dma_start(w_raw[:, 1], w_rows[1])
-        for z in range(PASSES):
-            nc.sync.dma_start(word_win[z][:], x_words[z].rearrange("p c r -> p (c r)").bitcast(I32))
+        words = [x_words[z].rearrange("p c r -> p (c r)").bitcast(I32) for z in range(PASSES)]
+        nc.sync.dma_start(word_win[0][:], words[0])
+        nc.sync.dma_start(word_win[1][:, 0:EARLY], words[1][:, 0:EARLY])
 
         nc.vector.tensor_copy(scale_got[:], scale_win[:].indirect(offsets[:]))
         for q in range(4):
-            nc.scalar.dma_start(
+            nc.sync.dma_start(
                 x_planes[32 * q : 32 * q + 4, :].bitcast(I32),
                 scale_got[32 * q : 32 * q + 32 : 4, :].bitcast(I32),
             )
+        nc.sync.dma_start(word_win[1][:, EARLY:T], words[1][:, EARLY:T])
 
         w_bf = keep.tile([P, PASSES, N, PACK], BF16, name="w_bf", align_bytes=64)
         w_codes = keep.tile([P, PASSES * N], U32, name="w_codes", align_bytes=64)

@@ -19,7 +19,7 @@ P = 128
 PACK = 4
 PASSES = K // (P * PACK)
 HALF = S // 2
-EARLY = 3 * T // 4
+EARLY = T // 2
 
 
 def tile_picked_phout_none_p_kernel(tc, x_words, x_scales, w1, res, gate, offs, out):

@@ -71,7 +71,8 @@ def tile_picked_phout_none_p_kernel(tc, x_words, x_scales, w1, res, gate, offs, 
 
         res_gate = keep.tile([P, S + 8], F32, name="res_gate", tag="stage")
         nc.sync.dma_start(res_gate[:, S : S + 1], gate)
-        nc.sync.dma_start(res_gate[:, 0:S], res)
+        for h in range(2):
+            nc.sync.dma_start(res_gate[:, h * HALF : (h + 1) * HALF], res[:, h * HALF : (h + 1) * HALF])
 
         got0 = keep.tile([P, S], U32, name="got0", align_bytes=64)
         got1 = [keep.tile([P, HALF], U32, name="got1_%d" % h, align_bytes=64) for h in range(2)]
@@ -98,5 +99,4 @@ def tile_picked_phout_none_p_kernel(tc, x_words, x_scales, w1, res, gate, offs, 
         for h in range(2):
             cols = slice(h * HALF, (h + 1) * HALF)
             nc.vector.scalar_tensor_tensor(result[h][:], acc[h][:], res_gate[:, S : S + 1], res_gate[:, cols], MULT, ADD)
-            queue = nc.sync if h == 0 else nc.scalar
-            queue.dma_start(out[:, cols], result[h][:])
+            nc.sync.dma_start(out[:, cols], result[h][:])

@@ -19,7 +19,6 @@ P = 128
 PACK = 4
 PASSES = K // (P * PACK)
 HALF = S // 2
-EARLY = T // 2
 
 
 def tile_picked_phout_none_p_kernel(tc, x_words, x_scales, w1, res, gate, offs, out):
@@ -33,31 +32,31 @@ def tile_picked_phout_none_p_kernel(tc, x_words, x_scales, w1, res, gate, offs, 
         word_win = [keep.tile([P, T], I32, name="word_win%d" % z, align_bytes=64) for z in range(PASSES)]
         scale_win = keep.tile([P, T], U8, name="scale_win", align_bytes=64)
         scale_got = keep.tile([P, S], U8, name="scale_got", align_bytes=64)
-        x_planes = keep.tile([P, PASSES * S], U8, name="x_planes", align_bytes=64)
+        x_planes = [keep.tile([P, S], U8, name="x_planes%d" % z, align_bytes=64) for z in range(PASSES)]
 
         nc.vector.memset(scale_win[:, 0 : T // 2].bitcast(I32), 0)
         nc.gpsimd.memset(scale_win[:, T // 2 : T].bitcast(I32), 0)
-        nc.vector.memset(x_planes[:].bitcast(I32), 0)
 
         w_rows = w1.rearrange("(z p j) m -> z p j m", z=PASSES, j=PACK)
         nc.sync.dma_start(w_raw[:, 0], w_rows[0])
         nc.sync.dma_start(offsets[:], offs)
-        nc.sync.dma_start(
-            scale_win[0:P:4, :].bitcast(I32),
-            x_scales.bitcast(I32).rearrange("z q c -> q z c"),
-        )
+        scale_rows = x_scales.bitcast(I32).rearrange("z (r b) c -> b r z c", b=2)
+        for b in range(2):
+            nc.sync.dma_start(scale_win[b:P:8, :].bitcast(I32), scale_rows[b])
         nc.sync.dma_start(w_raw[:, 1], w_rows[1])
         words = [x_words[z].rearrange("p c r -> p (c r)").bitcast(I32) for z in range(PASSES)]
-        nc.sync.dma_start(word_win[0][:], words[0])
-        nc.sync.dma_start(word_win[1][:, 0:EARLY], words[1][:, 0:EARLY])
+        for z in range(PASSES):
+            nc.sync.dma_start(word_win[z][:], words[z])
 
         nc.vector.tensor_copy(scale_got[:], scale_win[:].indirect(offsets[:]))
-        for q in range(4):
-            nc.sync.dma_start(
-                x_planes[32 * q : 32 * q + 4, :].bitcast(I32),
-                scale_got[32 * q : 32 * q + 32 : 4, :].bitcast(I32),
-            )
-        nc.sync.dma_start(word_win[1][:, EARLY:T], words[1][:, EARLY:T])
+        for z in range(PASSES):
+            nc.vector.tensor_copy(x_planes[z][:].bitcast(I32), scale_got[:].bitcast(I32))
+        for z in range(PASSES):
+            for b in range(2):
+                nc.sync.dma_start(
+                    x_planes[z][8 * z + 2 + b : P : 32, :].bitcast(I32),
+                    scale_got[16 + 8 * z + b : P : 32, :].bitcast(I32),
+                )
 
         w_bf = keep.tile([P, PASSES, N, PACK], BF16, name="w_bf", align_bytes=64)
         w_codes = keep.tile([P, PASSES * N], U32, name="w_codes", align_bytes=64)
@@ -92,7 +91,7 @@ def tile_picked_phout_none_p_kernel(tc, x_words, x_scales, w1, res, gate, offs, 
                     lhsT=w_codes[:, z * N : (z + 1) * N].bitcast(FP8X4),
                     lhsT_scale=w_planes[:, z * N : (z + 1) * N],
                     rhs=codes.bitcast(FP8X4),
-                    rhs_scale=x_planes[:, z * S + h * HALF : z * S + (h + 1) * HALF],
+                    rhs_scale=x_planes[z][8 * z : P, h * HALF : (h + 1) * HALF],
                     start=(z == 0),
                     stop=(z == PASSES - 1),
                 )

@@ -19,6 +19,7 @@ P = 128
 PACK = 4
 PASSES = K // (P * PACK)
 HALF = S // 2
+QUARTER = S // 4
 
 
 def tile_picked_phout_none_p_kernel(tc, x_words, x_scales, w1, res, gate, offs, out):
@@ -75,7 +76,8 @@ def tile_picked_phout_none_p_kernel(tc, x_words, x_scales, w1, res, gate, offs, 
 
         got0 = keep.tile([P, S], U32, name="got0", align_bytes=64)
         got1 = [keep.tile([P, HALF], U32, name="got1_%d" % h, align_bytes=64) for h in range(2)]
-        acc = [psum.tile([P, HALF], F32, name="acc%d" % h) for h in range(2)]
+        pieces = [(0, 0, HALF), (1, 0, QUARTER), (1, QUARTER, HALF)]
+        acc = [psum.tile([P, hi - lo], F32, name="acc%d" % i) for i, (h, lo, hi) in enumerate(pieces)]
         result = [keep.tile([P, HALF], F32, name="result%d" % h) for h in range(2)]
 
         nc.vector.tensor_copy(got0[:], word_win[0][:].bitcast(U32).indirect(offsets[:]))
@@ -84,18 +86,21 @@ def tile_picked_phout_none_p_kernel(tc, x_words, x_scales, w1, res, gate, offs, 
                 got1[h][:], word_win[1][:].bitcast(U32).indirect(offsets[:, h * 16 : (h + 1) * 16])
             )
         for z in range(PASSES):
-            for h in range(2):
-                codes = got0[:, h * HALF : (h + 1) * HALF] if z == 0 else got1[h][:]
+            for i, (h, lo, hi) in enumerate(pieces):
+                codes = got0[:, h * HALF + lo : h * HALF + hi] if z == 0 else got1[h][:, lo:hi]
                 nc.tensor.matmul_mx(
-                    out=acc[h][:],
+                    out=acc[i][:],
                     lhsT=w_codes[:, z * N : (z + 1) * N].bitcast(FP8X4),
                     lhsT_scale=w_planes[:, z * N : (z + 1) * N],
                     rhs=codes.bitcast(FP8X4),
-                    rhs_scale=x_planes[z][8 * z : P, h * HALF : (h + 1) * HALF],
+                    rhs_scale=x_planes[z][8 * z : P, h * HALF + lo : h * HALF + hi],
                     start=(z == 0),
                     stop=(z == PASSES - 1),
                 )
-        for h in range(2):
-            cols = slice(h * HALF, (h + 1) * HALF)
-            nc.vector.scalar_tensor_tensor(result[h][:], acc[h][:], res_gate[:, S : S + 1], res_gate[:, cols], MULT, ADD)
-            nc.sync.dma_start(out[:, cols], result[h][:])
+        for i, (h, lo, hi) in enumerate(pieces):
+            cols = slice(h * HALF + lo, h * HALF + hi)
+            nc.vector.scalar_tensor_tensor(
+                result[h][:, lo:hi], acc[i][:], res_gate[:, S : S + 1], res_gate[:, cols], MULT, ADD
+            )
+            if hi == HALF:
+                nc.sync.dma_start(out[:, h * HALF : (h + 1) * HALF], result[h][:])

@@ -31,20 +31,18 @@ def tile_picked_phout_none_p_kernel(tc, x_words, x_scales, w1, res, gate, offs, 
         offsets = keep.tile([P, S // 16], U16, name="offsets")
         w_raw = keep.tile([P, PASSES, PACK, N], F32, name="w_raw", tag="stage")
         word_win = [keep.tile([P, T], I32, name="word_win%d" % z, align_bytes=64) for z in range(PASSES)]
-        scale_win = keep.tile([P, T], U8, name="scale_win", align_bytes=64)
+        scale_win = keep.tile([P, T], U8, name="scale_win", tag="early", align_bytes=64)
         scale_got = keep.tile([P, S], U8, name="scale_got", align_bytes=64)
         x_planes = [keep.tile([P, S], U8, name="x_planes%d" % z, align_bytes=64) for z in range(PASSES)]
 
         nc.vector.memset(scale_win[:, 0 : T // 2].bitcast(I32), 0)
         nc.gpsimd.memset(scale_win[:, T // 2 : T].bitcast(I32), 0)
 
-        w_rows = w1.rearrange("(z p j) m -> z p j m", z=PASSES, j=PACK)
-        nc.sync.dma_start(w_raw[:, 0], w_rows[0])
+        nc.sync.dma_start(w_raw[:], w1.rearrange("(z p j) m -> p z j m", z=PASSES, j=PACK))
         nc.sync.dma_start(offsets[:], offs)
         scale_rows = x_scales.bitcast(I32).rearrange("z (r b) c -> b r z c", b=2)
         for b in range(2):
             nc.sync.dma_start(scale_win[b:P:8, :].bitcast(I32), scale_rows[b])
-        nc.sync.dma_start(w_raw[:, 1], w_rows[1])
         words = [x_words[z].rearrange("p c r -> p (c r)").bitcast(I32) for z in range(PASSES)]
         for z in range(PASSES):
             nc.sync.dma_start(word_win[z][:], words[z])
@@ -59,7 +57,7 @@ def tile_picked_phout_none_p_kernel(tc, x_words, x_scales, w1, res, gate, offs, 
                     scale_got[16 + 8 * z + b : P : 32, :].bitcast(I32),
                 )
 
-        w_bf = keep.tile([P, PASSES, N, PACK], BF16, name="w_bf", align_bytes=64)
+        w_bf = keep.tile([P, PASSES, N, PACK], BF16, name="w_bf", tag="early", align_bytes=64)
         w_codes = keep.tile([P, PASSES * N], U32, name="w_codes", align_bytes=64)
         w_planes = keep.tile([P, PASSES * N], U8, name="w_planes", align_bytes=64)
         nc.vector.tensor_copy(w_bf[:], w_raw[:].rearrange("p z j m -> p z m j"))
@@ -78,7 +76,7 @@ def tile_picked_phout_none_p_kernel(tc, x_words, x_scales, w1, res, gate, offs, 
         got1 = [keep.tile([P, HALF], U32, name="got1_%d" % h, align_bytes=64) for h in range(2)]
         pieces = [(0, 0, HALF), (1, 0, QUARTER), (1, QUARTER, HALF)]
         acc = [psum.tile([P, hi - lo], F32, name="acc%d" % i) for i, (h, lo, hi) in enumerate(pieces)]
-        result = [keep.tile([P, HALF], F32, name="result%d" % h) for h in range(2)]
+        result = [keep.tile([P, hi - lo], F32, name="result%d" % i) for i, (h, lo, hi) in enumerate(pieces)]
 
         nc.vector.tensor_copy(got0[:], word_win[0][:].bitcast(U32).indirect(offsets[:]))
         for h in range(2):
@@ -100,7 +98,6 @@ def tile_picked_phout_none_p_kernel(tc, x_words, x_scales, w1, res, gate, offs, 
         for i, (h, lo, hi) in enumerate(pieces):
             cols = slice(h * HALF + lo, h * HALF + hi)
             nc.vector.scalar_tensor_tensor(
-                result[h][:, lo:hi], acc[i][:], res_gate[:, S : S + 1], res_gate[:, cols], MULT, ADD
+                result[i][:], acc[i][:], res_gate[:, S : S + 1], res_gate[:, cols], MULT, ADD
             )
-            if hi == HALF:
-                nc.sync.dma_start(out[:, h * HALF : (h + 1) * HALF], result[h][:])
+            nc.sync.dma_start(out[:, cols], result[i][:])

@@ -30,7 +30,7 @@ def tile_picked_phout_none_p_kernel(tc, x_words, x_scales, w1, res, gate, offs, 
 
         offsets = keep.tile([P, S // 16], U16, name="offsets")
         w_raw = keep.tile([P, PASSES, PACK, N], F32, name="w_raw", tag="stage")
-        word_win = [keep.tile([P, T], I32, name="word_win%d" % z, align_bytes=64) for z in range(PASSES)]
+        word_win = [keep.tile([P, T], I32, name="word_win%d" % z, tag="win%d" % z, align_bytes=64) for z in range(PASSES)]
         scale_win = keep.tile([P, T], U8, name="scale_win", tag="early", align_bytes=64)
         scale_got = keep.tile([P, S], U8, name="scale_got", align_bytes=64)
         x_planes = [keep.tile([P, S], U8, name="x_planes%d" % z, align_bytes=64) for z in range(PASSES)]
@@ -57,28 +57,32 @@ def tile_picked_phout_none_p_kernel(tc, x_words, x_scales, w1, res, gate, offs, 
                     scale_got[16 + 8 * z + b : P : 32, :].bitcast(I32),
                 )
 
-        w_bf = keep.tile([P, PASSES, N, PACK], BF16, name="w_bf", tag="early", align_bytes=64)
+        w_bf = keep.tile([P, PASSES, N, PACK], BF16, name="w_bf", tag="got", align_bytes=64)
         w_codes = keep.tile([P, PASSES * N], U32, name="w_codes", align_bytes=64)
         w_planes = keep.tile([P, PASSES * N], U8, name="w_planes", align_bytes=64)
-        nc.vector.tensor_copy(w_bf[:], w_raw[:].rearrange("p z j m -> p z m j"))
+        for z in range(PASSES):
+            nc.scalar.copy(
+                w_bf[:, z].rearrange("p (c i) j -> p c j i", i=4), w_raw[:, z].rearrange("p j (c i) -> p c j i", i=4)
+            )
         nc.vector.quantize_mx(
             out=w_codes[:].bitcast(FP8X4),
             scales=w_planes[:],
             in_=w_bf[:].rearrange("p z m j -> p (z m j)"),
         )
 
-        res_gate = keep.tile([P, S + 8], F32, name="res_gate", tag="stage")
-        nc.sync.dma_start(res_gate[:, S : S + 1], gate)
-        for h in range(2):
-            nc.sync.dma_start(res_gate[:, h * HALF : (h + 1) * HALF], res[:, h * HALF : (h + 1) * HALF])
-
-        got0 = keep.tile([P, S], U32, name="got0", align_bytes=64)
+        got0 = keep.tile([P, S], U32, name="got0", tag="got", align_bytes=64)
         got1 = [keep.tile([P, HALF], U32, name="got1_%d" % h, align_bytes=64) for h in range(2)]
         pieces = [(0, 0, HALF), (1, 0, QUARTER), (1, QUARTER, HALF)]
         acc = [psum.tile([P, hi - lo], F32, name="acc%d" % i) for i, (h, lo, hi) in enumerate(pieces)]
         result = [keep.tile([P, hi - lo], F32, name="result%d" % i) for i, (h, lo, hi) in enumerate(pieces)]
 
         nc.vector.tensor_copy(got0[:], word_win[0][:].bitcast(U32).indirect(offsets[:]))
+        gate_col = keep.tile([P, 1], F32, name="gate_col", tag="stage")
+        nc.sync.dma_start(gate_col[:], gate)
+        res_gate = keep.tile([P, S], F32, name="res_gate", tag="win0", align_bytes=64)
+        for h in range(2):
+            nc.sync.dma_start(res_gate[:, h * HALF : (h + 1) * HALF], res[:, h * HALF : (h + 1) * HALF])
+
         for h in range(2):
             nc.vector.tensor_copy(
                 got1[h][:], word_win[1][:].bitcast(U32).indirect(offsets[:, h * 16 : (h + 1) * 16])
@@ -98,6 +102,6 @@ def tile_picked_phout_none_p_kernel(tc, x_words, x_scales, w1, res, gate, offs, 
         for i, (h, lo, hi) in enumerate(pieces):
             cols = slice(h * HALF + lo, h * HALF + hi)
             nc.vector.scalar_tensor_tensor(
-                result[i][:], acc[i][:], res_gate[:, S : S + 1], res_gate[:, cols], MULT, ADD
+                result[i][:], acc[i][:], gate_col[:], res_gate[:, cols], MULT, ADD
             )
             nc.sync.dma_start(out[:, cols], result[i][:])

@@ -26,6 +26,7 @@ def tile_picked_phout_none_p_kernel(tc, x_words, x_scales, w1, res, gate, offs, 
     nc = tc.nc
     with ExitStack() as ctx:
         keep = ctx.enter_context(tc.tile_pool(name="keep", bufs=1))
+        outp = ctx.enter_context(tc.tile_pool(name="outp", bufs=1))
         psum = ctx.enter_context(tc.psum_pool(name="psum", bufs=1))
 
         offsets = keep.tile([P, S // 16], U16, name="offsets")
@@ -74,7 +75,9 @@ def tile_picked_phout_none_p_kernel(tc, x_words, x_scales, w1, res, gate, offs, 
         got1 = [keep.tile([P, HALF], U32, name="got1_%d" % h, align_bytes=64) for h in range(2)]
         pieces = [(0, 0, HALF), (1, 0, QUARTER), (1, QUARTER, HALF)]
         acc = [psum.tile([P, hi - lo], F32, name="acc%d" % i) for i, (h, lo, hi) in enumerate(pieces)]
-        result = [keep.tile([P, hi - lo], F32, name="result%d" % i) for i, (h, lo, hi) in enumerate(pieces)]
+        result = [
+            outp.tile([P, hi - lo], F32, name="result%d" % i, align_bytes=256) for i, (h, lo, hi) in enumerate(pieces)
+        ]
 
         nc.vector.tensor_copy(got0[:], word_win[0][:].bitcast(U32).indirect(offsets[:]))
         gate_col = keep.tile([P, 1], F32, name="gate_col", tag="stage")

@@ -61,10 +61,8 @@ def tile_picked_phout_none_p_kernel(tc, x_words, x_scales, w1, res, gate, offs, 
         w_bf = keep.tile([P, PASSES, N, PACK], BF16, name="w_bf", tag="got", align_bytes=64)
         w_codes = keep.tile([P, PASSES * N], U32, name="w_codes", align_bytes=64)
         w_planes = keep.tile([P, PASSES * N], U8, name="w_planes", align_bytes=64)
-        for z in range(PASSES):
-            nc.scalar.copy(
-                w_bf[:, z].rearrange("p (c i) j -> p c j i", i=4), w_raw[:, z].rearrange("p j (c i) -> p c j i", i=4)
-            )
+        for z, cast in enumerate((nc.scalar.copy, nc.vector.tensor_copy)):
+            cast(w_bf[:, z].rearrange("p (c i) j -> p c j i", i=4), w_raw[:, z].rearrange("p j (c i) -> p c j i", i=4))
         nc.vector.quantize_mx(
             out=w_codes[:].bitcast(FP8X4),
             scales=w_planes[:],

@@ -30,7 +30,7 @@ def tile_picked_phout_none_p_kernel(tc, x_words, x_scales, w1, res, gate, offs, 
         psum = ctx.enter_context(tc.psum_pool(name="psum", bufs=1))
 
         offsets = keep.tile([P, S // 16], U16, name="offsets")
-        w_raw = keep.tile([P, PASSES, PACK, N], F32, name="w_raw", tag="stage")
+        w_raw = outp.tile([P, PASSES, PACK, N], F32, name="w_raw", tag="stage", align_bytes=256)
         word_win = [keep.tile([P, T], I32, name="word_win%d" % z, tag="win%d" % z, align_bytes=64) for z in range(PASSES)]
         scale_win = keep.tile([P, T], U8, name="scale_win", tag="early", align_bytes=64)
         scale_got = keep.tile([P, S], U8, name="scale_got", align_bytes=64)
@@ -78,7 +78,7 @@ def tile_picked_phout_none_p_kernel(tc, x_words, x_scales, w1, res, gate, offs, 
         ]
 
         nc.vector.tensor_copy(got0[:], word_win[0][:].bitcast(U32).indirect(offsets[:]))
-        gate_col = keep.tile([P, 1], F32, name="gate_col", tag="stage")
+        gate_col = outp.tile([P, 1], F32, name="gate_col", tag="stage", align_bytes=256)
         nc.sync.dma_start(gate_col[:], gate)
         res_gate = keep.tile([P, S], F32, name="res_gate", tag="win0", align_bytes=64)
         for h in range(2):

@@ -33,8 +33,8 @@ def tile_picked_phout_none_p_kernel(tc, x_words, x_scales, w1, res, gate, offs, 
         w_raw = outp.tile([P, PASSES, PACK, N], F32, name="w_raw", tag="stage", align_bytes=256)
         word_win = [keep.tile([P, T], I32, name="word_win%d" % z, tag="win%d" % z, align_bytes=64) for z in range(PASSES)]
         scale_win = keep.tile([P, T], U8, name="scale_win", tag="early", align_bytes=64)
-        scale_got = keep.tile([P, S], U8, name="scale_got", align_bytes=64)
-        x_planes = [keep.tile([P, S], U8, name="x_planes%d" % z, align_bytes=64) for z in range(PASSES)]
+        scale_got = keep.tile([P, S], U8, name="scale_got", align_bytes=256)
+        x_planes = [keep.tile([P, S], U8, name="x_planes%d" % z, align_bytes=256) for z in range(PASSES)]
 
         nc.vector.memset(scale_win[:, 0 : T // 2].bitcast(I32), 0)
         nc.gpsimd.memset(scale_win[:, T // 2 : T].bitcast(I32), 0)
@@ -58,9 +58,9 @@ def tile_picked_phout_none_p_kernel(tc, x_words, x_scales, w1, res, gate, offs, 
                     scale_got[16 + 8 * z + b : P : 32, :].bitcast(I32),
                 )
 
-        w_bf = keep.tile([P, PASSES, N, PACK], BF16, name="w_bf", tag="got", align_bytes=64)
-        w_codes = keep.tile([P, PASSES * N], U32, name="w_codes", align_bytes=64)
-        w_planes = keep.tile([P, PASSES * N], U8, name="w_planes", align_bytes=64)
+        w_bf = keep.tile([P, PASSES, N, PACK], BF16, name="w_bf", tag="got", align_bytes=256)
+        w_codes = keep.tile([P, PASSES * N], U32, name="w_codes", align_bytes=256)
+        w_planes = keep.tile([P, PASSES * N], U8, name="w_planes", align_bytes=256)
         for z, cast in enumerate((nc.scalar.copy, nc.vector.tensor_copy)):
             cast(w_bf[:, z].rearrange("p (c i) j -> p c j i", i=4), w_raw[:, z].rearrange("p j (c i) -> p c j i", i=4))
         nc.vector.quantize_mx(
@@ -69,8 +69,8 @@ def tile_picked_phout_none_p_kernel(tc, x_words, x_scales, w1, res, gate, offs, 
             in_=w_bf[:].rearrange("p z m j -> p (z m j)"),
         )
 
-        got0 = keep.tile([P, S], U32, name="got0", tag="got", align_bytes=64)
-        got1 = [keep.tile([P, HALF], U32, name="got1_%d" % h, align_bytes=64) for h in range(2)]
+        got0 = keep.tile([P, S], U32, name="got0", tag="got", align_bytes=256)
+        got1 = [keep.tile([P, HALF], U32, name="got1_%d" % h, align_bytes=256) for h in range(2)]
         pieces = [(0, 0, HALF), (1, 0, QUARTER), (1, QUARTER, HALF)]
         acc = [psum.tile([P, hi - lo], F32, name="acc%d" % i) for i, (h, lo, hi) in enumerate(pieces)]
         result = [

@@ -27,12 +27,16 @@ def tile_picked_phout_none_p_kernel(tc, x_words, x_scales, w1, res, gate, offs, 
     with ExitStack() as ctx:
         keep = ctx.enter_context(tc.tile_pool(name="keep", bufs=1))
         outp = ctx.enter_context(tc.tile_pool(name="outp", bufs=1))
+        wins = ctx.enter_context(tc.tile_pool(name="wins", bufs=1))
         psum = ctx.enter_context(tc.psum_pool(name="psum", bufs=1))
 
         offsets = keep.tile([P, S // 16], U16, name="offsets")
         w_raw = outp.tile([P, PASSES, PACK, N], F32, name="w_raw", tag="stage", align_bytes=256)
-        word_win = [keep.tile([P, T], I32, name="word_win%d" % z, tag="win%d" % z, align_bytes=64) for z in range(PASSES)]
-        scale_win = keep.tile([P, T], U8, name="scale_win", tag="early", align_bytes=64)
+        word_win = [
+            wins.tile([P, T], I32, name="word_win0", offset=4 * T + 32),
+            wins.tile([P, T], I32, name="word_win1", offset=0, align_bytes=256),
+        ]
+        scale_win = keep.tile([P, T], U8, name="scale_win", align_bytes=256)
         scale_got = keep.tile([P, S], U8, name="scale_got", align_bytes=256)
         x_planes = [keep.tile([P, S], U8, name="x_planes%d" % z, align_bytes=256) for z in range(PASSES)]
 
@@ -80,7 +84,7 @@ def tile_picked_phout_none_p_kernel(tc, x_words, x_scales, w1, res, gate, offs, 
         nc.vector.tensor_copy(got0[:], word_win[0][:].bitcast(U32).indirect(offsets[:]))
         gate_col = outp.tile([P, 1], F32, name="gate_col", tag="stage", align_bytes=256)
         nc.sync.dma_start(gate_col[:], gate)
-        res_gate = keep.tile([P, S], F32, name="res_gate", tag="win0", align_bytes=64)
+        res_gate = wins.tile([P, S], F32, name="res_gate", offset=4 * T + 32)
         for h in range(2):
             nc.sync.dma_start(res_gate[:, h * HALF : (h + 1) * HALF], res[:, h * HALF : (h + 1) * HALF])
 

@@ -30,7 +30,7 @@ def tile_picked_phout_none_p_kernel(tc, x_words, x_scales, w1, res, gate, offs, 
         wins = ctx.enter_context(tc.tile_pool(name="wins", bufs=1))
         psum = ctx.enter_context(tc.psum_pool(name="psum", bufs=1))
 
-        offsets = keep.tile([P, S // 16], U16, name="offsets")
+        offsets = keep.tile([P, S // 16], U16, name="offsets", align_bytes=256)
         w_raw = outp.tile([P, PASSES, PACK, N], F32, name="w_raw", tag="stage", align_bytes=256)
         word_win = [
             wins.tile([P, T], I32, name="word_win0", offset=4 * T + 32),

from contextlib import ExitStack

import concourse.mybir as mybir

K, T, S, N = 1024, 2048, 512, 128
FLOPS = 2 * K * S * N

F32 = mybir.dt.float32
BF16 = mybir.dt.bfloat16
I32 = mybir.dt.int32
U32 = mybir.dt.uint32
U16 = mybir.dt.uint16
U8 = mybir.dt.uint8
FP8X4 = mybir.dt.float8_e4m3fn_x4
MULT = mybir.AluOpType.mult
ADD = mybir.AluOpType.add

P = 128
PACK = 4
PASSES = K // (P * PACK)
HALF = S // 2
QUARTER = S // 4


def tile_picked_phout_none_p_kernel(tc, x_words, x_scales, w1, res, gate, offs, out):
    nc = tc.nc
    with ExitStack() as ctx:
        keep = ctx.enter_context(tc.tile_pool(name="keep", bufs=1))
        outp = ctx.enter_context(tc.tile_pool(name="outp", bufs=1))
        wins = ctx.enter_context(tc.tile_pool(name="wins", bufs=1))
        psum = ctx.enter_context(tc.psum_pool(name="psum", bufs=1))

        offsets = keep.tile([P, S // 16], U16, name="offsets", align_bytes=256)
        w_raw = outp.tile([P, PASSES, PACK, N], F32, name="w_raw", tag="stage", align_bytes=256)
        word_win = [
            wins.tile([P, T], I32, name="word_win0", offset=4 * T + 32),
            wins.tile([P, T], I32, name="word_win1", offset=0, align_bytes=256),
        ]
        scale_win = keep.tile([P, T], U8, name="scale_win", align_bytes=256)
        scale_got = keep.tile([P, S], U8, name="scale_got", align_bytes=256)
        x_planes = [keep.tile([P, S], U8, name="x_planes%d" % z, align_bytes=256) for z in range(PASSES)]

        nc.vector.memset(scale_win[:, 0 : T // 2].bitcast(I32), 0)
        nc.gpsimd.memset(scale_win[:, T // 2 : T].bitcast(I32), 0)

        nc.sync.dma_start(w_raw[:], w1.rearrange("(z p j) m -> p z j m", z=PASSES, j=PACK))
        nc.sync.dma_start(offsets[:], offs)
        scale_rows = x_scales.bitcast(I32).rearrange("z (r b) c -> b r z c", b=2)
        for b in range(2):
            nc.sync.dma_start(scale_win[b:P:8, :].bitcast(I32), scale_rows[b])
        words = [x_words[z].rearrange("p c r -> p (c r)").bitcast(I32) for z in range(PASSES)]
        for z in range(PASSES):
            nc.sync.dma_start(word_win[z][:], words[z])

        nc.vector.tensor_copy(scale_got[:], scale_win[:].indirect(offsets[:]))
        for z in range(PASSES):
            nc.vector.tensor_copy(x_planes[z][:].bitcast(I32), scale_got[:].bitcast(I32))
        for z in range(PASSES):
            for b in range(2):
                nc.sync.dma_start(
                    x_planes[z][8 * z + 2 + b : P : 32, :].bitcast(I32),
                    scale_got[16 + 8 * z + b : P : 32, :].bitcast(I32),
                )

        w_bf = keep.tile([P, PASSES, N, PACK], BF16, name="w_bf", tag="got", align_bytes=256)
        w_codes = keep.tile([P, PASSES * N], U32, name="w_codes", align_bytes=256)
        w_planes = keep.tile([P, PASSES * N], U8, name="w_planes", align_bytes=256)
        for z, cast in enumerate((nc.scalar.copy, nc.vector.tensor_copy)):
            cast(w_bf[:, z].rearrange("p (c i) j -> p c j i", i=4), w_raw[:, z].rearrange("p j (c i) -> p c j i", i=4))
        nc.vector.quantize_mx(
            out=w_codes[:].bitcast(FP8X4),
            scales=w_planes[:],
            in_=w_bf[:].rearrange("p z m j -> p (z m j)"),
        )

        got0 = keep.tile([P, S], U32, name="got0", tag="got", align_bytes=256)
        got1 = [keep.tile([P, HALF], U32, name="got1_%d" % h, align_bytes=256) for h in range(2)]
        pieces = [(0, 0, HALF), (1, 0, QUARTER), (1, QUARTER, HALF)]
        acc = [psum.tile([P, hi - lo], F32, name="acc%d" % i) for i, (h, lo, hi) in enumerate(pieces)]
        result = [
            outp.tile([P, hi - lo], F32, name="result%d" % i, align_bytes=256) for i, (h, lo, hi) in enumerate(pieces)
        ]

        nc.vector.tensor_copy(got0[:], word_win[0][:].bitcast(U32).indirect(offsets[:]))
        gate_col = outp.tile([P, 1], F32, name="gate_col", tag="stage", align_bytes=256)
        nc.sync.dma_start(gate_col[:], gate)
        res_gate = wins.tile([P, S], F32, name="res_gate", offset=4 * T + 32)
        for h in range(2):
            nc.sync.dma_start(res_gate[:, h * HALF : (h + 1) * HALF], res[:, h * HALF : (h + 1) * HALF])

        for h in range(2):
            nc.vector.tensor_copy(
                got1[h][:], word_win[1][:].bitcast(U32).indirect(offsets[:, h * 16 : (h + 1) * 16])
            )
        for z in range(PASSES):
            for i, (h, lo, hi) in enumerate(pieces):
                codes = got0[:, h * HALF + lo : h * HALF + hi] if z == 0 else got1[h][:, lo:hi]
                nc.tensor.matmul_mx(
                    out=acc[i][:],
                    lhsT=w_codes[:, z * N : (z + 1) * N].bitcast(FP8X4),
                    lhsT_scale=w_planes[:, z * N : (z + 1) * N],
                    rhs=codes.bitcast(FP8X4),
                    rhs_scale=x_planes[z][8 * z : P, h * HALF + lo : h * HALF + hi],
                    start=(z == 0),
                    stop=(z == PASSES - 1),
                )
        for i, (h, lo, hi) in enumerate(pieces):
            cols = slice(h * HALF + lo, h * HALF + hi)
            nc.vector.scalar_tensor_tensor(
                result[i][:], acc[i][:], gate_col[:], res_gate[:, cols], MULT, ADD
            )
            nc.sync.dma_start(out[:, cols], result[i][:])
